import numpy as np
import ml_dtypes


def mxq(x, axis, fmt="e4m3"):
    dtype, down = {"e4m3": (ml_dtypes.float8_e4m3fn, 7), "e5m2": (ml_dtypes.float8_e5m2, 14)}[fmt]
    v = np.moveaxis(np.asarray(x, np.float32).astype(ml_dtypes.bfloat16).astype(np.float64), axis, -1)
    blocks = v.reshape(v.shape[:-1] + (-1, 32))
    amax = np.abs(blocks).max(-1, keepdims=True)
    byte = np.maximum(np.where(amax > 0, np.frexp(amax)[1] - 1 + 127, 0) - down, 1)
    scale = np.exp2(byte - 127.0)
    codes = (blocks / scale).astype(np.float32).astype(dtype).astype(np.float64)
    return np.moveaxis((codes * scale).reshape(v.shape), -1, axis)


WIDE = False


def mx_kscale(k):
    if not WIDE:
        return np.ones(k)
    levels = np.array([10, -10, 5, -5, 0])
    if k % 512:
        return np.exp2(np.random.permutation(np.resize(levels, k // 32))).repeat(32)
    a = np.empty((k // 512, 16))
    for p in range(k // 512):
        a[p, :8] = np.random.permutation(np.resize(levels, 8))
        for g in range(8):
            far = levels[np.abs(levels - a[p, g]) >= 10]
            a[p, g + 8] = far[np.random.randint(len(far))]
    return np.exp2(a.ravel()).repeat(32)


def f64(x):
    return np.asarray(x).astype(np.float64)


def striped(idx):
    return np.tile(np.asarray(idx).reshape(-1, 16).T, (8, 1)).astype(np.uint16)


def unstriped(offs):
    return offs[:16].T.reshape(-1).astype(np.int64)


E2M1 = np.array([0.0, 0.5, 1.0, 1.5, 2.0, 3.0, 4.0, 6.0, -0.0, -0.5, -1.0, -1.5, -2.0, -3.0, -4.0, -6.0])


def pack_weight(w, fmt):
    k, n = w.shape
    w = f64(np.asarray(w, np.float32).astype(ml_dtypes.bfloat16)).reshape(k // 32, 32, n)
    amax = np.abs(w).max(1)
    if fmt == "e4m3":
        byte = np.frexp(amax)[1] - 1 + 127 - 7
    else:
        mant, ex = np.frexp(amax / 6.0)
        byte = np.where(mant > 0.5, ex, ex - 1) + 127
    byte = np.clip(np.where(amax > 0, byte, 1), 1, 254)
    scaled = (w * np.exp2(127.0 - byte)[:, None, :]).reshape(k, n).astype(np.float32)
    by_word = np.ascontiguousarray(scaled.reshape(k // 512, 128, 4, n).transpose(0, 1, 3, 2))
    if fmt == "e4m3":
        words = by_word.astype(ml_dtypes.float8_e4m3fn).view(np.uint8)
    else:
        c = by_word.astype(ml_dtypes.float4_e2m1fn).view(np.uint8) & 0xF
        words = (c[..., 0::2] | (c[..., 1::2] << 4)).reshape(k // 512, 128, 2 * n)
    return np.ascontiguousarray(words), np.ascontiguousarray(byte.astype(np.uint8).reshape(k // 512, 16, n))


def unpack_weight(words, scales, fmt):
    g, _, n = scales.shape
    words = np.ascontiguousarray(words).reshape(g, 128, n, -1)
    if fmt == "e4m3":
        vals = words.view(ml_dtypes.float8_e4m3fn).astype(np.float64)
    else:
        nib = np.empty((g, 128, n, 4), np.uint8)
        nib[..., 0::2] = words & 0xF
        nib[..., 1::2] = words >> 4
        vals = E2M1[nib]
    vals = vals * np.repeat(np.exp2(scales.astype(np.float64) - 127.0), 8, axis=1)[..., None]
    return vals.transpose(0, 1, 3, 2).reshape(g * 512, n)


D, E, T, I, Q = 512, 512, 1024, 256, 512


def setup_inputs():
    n = np.random.standard_normal
    idx2 = np.random.permutation(I)[:I]
    idx = np.random.permutation(T)[:I]
    fd = mx_kscale(D)
    fq = mx_kscale(Q)
    keysp = pack_weight(n((D, T)) / fd[:, None], "e2m1")
    return {
        "query": (n((D, Q)) * 0.7 / np.sqrt(D) * fd[:, None]).astype(np.float32),
        "keys_words": keysp[0],
        "keys_scales": keysp[1],
        "qs": (np.random.uniform(2.0, 8.0, (Q, 1)) * fq[:, None]).astype(np.float32),
        "grows": (n((Q, E)) / fq[:, None]).astype(np.float32),
        "old": (n((E, T)) * 2.0).astype(np.float32),
        "fade": (np.random.uniform(0.5, 1.0, (1, T))).astype(np.float32),
        "offs2": striped(idx2),
        "offs": striped(idx),
    }


def reference(query, keys_words, keys_scales, qs, grows, old, fade, offs2, offs):
    idx2 = unstriped(offs2)
    idx = unstriped(offs)
    keysu = unpack_weight(keys_words, keys_scales, "e2m1")
    queryq = mxq(f64(query), 0, "e4m3")
    keysidxg = keysu[:, idx]
    a = queryq.T @ keysidxg
    pa = np.exp(a)
    pb = np.sqrt(pa)
    p = pa * pb[:, idx2]
    z = np.sum(p, axis=1, keepdims=True)
    w = p / z
    wq = w * f64(qs)
    growsq = mxq(f64(grows), 0, "e4m3")
    wqq = mxq(wq, 0, "e4m3")
    gv = growsq.T @ wqq
    gf = np.zeros((E, T))
    gf[:, idx] = gv
    y = f64(old) * f64(fade) + gf
    return y

@@ -1,0 +1,212 @@
+from contextlib import ExitStack
+
+import concourse.mybir as mybir
+from concourse.masks import make_identity
+
+F32 = mybir.dt.float32
+BF16 = mybir.dt.bfloat16
+I32 = mybir.dt.int32
+U32 = mybir.dt.uint32
+U16 = mybir.dt.uint16
+U8 = mybir.dt.uint8
+FP8X4 = mybir.dt.float8_e4m3fn_x4
+FP4X4 = mybir.dt.float4_e2m1fn_x4
+ALU = mybir.AluOpType
+ACT = mybir.ActivationFunctionType
+
+P = 128
+PACK = 4
+D, E, T, I, Q = 512, 512, 1024, 256, 512
+BANK = 512
+FLOPS = 2 * D * Q * I + 2 * Q * E * I
+
+
+def tile_attend_blinkedproduct_v_kernel(tc, query, keys_words, keys_scales, qs, grows, old, fade, offs2, offs, out):
+    nc = tc.nc
+    with ExitStack() as ctx:
+        lists = ctx.enter_context(tc.tile_pool(name="lists", bufs=1))
+        sb = ctx.enter_context(tc.tile_pool(name="sb", bufs=1))
+        ps = ctx.enter_context(tc.psum_pool(name="ps", bufs=1))
+
+        offs_sb = lists.tile([P, I // 16], U16, name="offs_sb")
+        offs2_sb = lists.tile([P, I // 16], U16, name="offs2_sb")
+        words = sb.tile([P, T], U16, name="words", tag="slot_a")
+        kscales = sb.tile([P, T], U8, name="kscales", tag="slot_b")
+        q_raw = sb.tile([P, PACK, Q], F32, name="q_raw", tag="slot_d")
+        qs_sb = sb.tile([P, PACK], F32, name="qs_sb")
+        fade8 = sb.tile([P, 8], F32, name="fade8", tag="slot_c")
+        fade_rows = sb.tile([P, P], F32, name="fade_rows")
+        ident = sb.tile([P, P], F32, name="ident")
+        gf = [sb.tile([P, T], F32, name=f"gf{j}") for j in range(4)]
+        warm = sb.tile([P, 1], F32, name="warm")
+
+        nc.gpsimd.memset(kscales[:].bitcast(I32), 0)
+        nc.sync.dma_start(offs_sb[:], offs)
+        nc.sync.dma_start(words[:].bitcast(I32), keys_words[0].bitcast(I32))
+        nc.sync.dma_start(q_raw[:], query.rearrange("(p j) q -> p j q", j=PACK))
+        nc.scalar.dma_start(fade8[:], fade.rearrange("o (p b) -> p (o b)", b=8))
+        for r in range(4):
+            nc.scalar.dma_start(kscales[r:P:32, :].bitcast(I32), keys_scales[0][r:16:4, :].bitcast(I32))
+        make_identity(nc, ident[:])
+        nc.gpsimd.memset(fade_rows[:], 0.0)
+        nc.scalar.activation(warm[:], ident[:, 0:1], ACT.Exp)
+        for j in range(4):
+            nc.vector.memset(gf[j][:], 0.0)
+        nc.sync.dma_start(offs2_sb[:], offs2)
+        nc.gpsimd.dma_start(fade_rows[0:8, :], fade.rearrange("o (b n) -> (o b) n", b=8))
+        nc.gpsimd.dma_start(qs_sb[:], qs.rearrange("(p j) o -> p (j o)", j=PACK))
+
+        fade_all = sb.tile([P, T], F32, name="fade_all")
+        fade_nb = fade_all[:].rearrange("p (n b) -> p n b", b=8)
+        for h in range(2):
+            bank = ps.tile([P, 4, P], F32, name=f"fade_bank{h}", tag=f"turn{h}")
+            for b in range(4):
+                col = fade8[:, 4 * h + b : 4 * h + b + 1]
+                nc.tensor.transpose(bank[:, b, :], col.to_broadcast([P, P]), ident[:])
+            nc.scalar.copy(fade_nb[:, :, 4 * h : 4 * h + 4], bank[:].rearrange("p b n -> p n b"))
+
+        k_words = sb.tile([P, I], U16, name="k_words", align_bytes=64)
+        k_scales = sb.tile([P, I], U8, name="k_scales", align_bytes=64)
+        nc.vector.tensor_copy(k_words[:], words[:].indirect(offs_sb[:]))
+        nc.vector.tensor_copy(k_scales[:], kscales[:].indirect(offs_sb[:]))
+
+        g_raw = sb.tile([P, PACK, E], F32, name="g_raw", tag="slot_a")
+        nc.sync.dma_start(g_raw[:], grows.rearrange("(p j) e -> p j e", j=PACK))
+        old_sb = {}
+
+        def load_old(j, tag, align):
+            old_sb[j] = sb.tile([P, T], F32, name=f"old{j}", tag=tag, align_bytes=align)
+            nc.sync.dma_start(old_sb[j][:], old[j * P : (j + 1) * P, :])
+
+        load_old(2, "slot_b", None)
+        load_old(3, "slot_c", None)
+
+        q_src = q_raw[:].rearrange("p j (s r) -> p s j r", r=PACK)
+        q_codes, q_scales, q_bf = [], [], []
+        for h in range(2):
+            q_bf.append(sb.tile([P, 2, P, PACK], BF16, name=f"q_bf{h}", tag=f"slot_q{h}", align_bytes=64))
+            q_codes.append(sb.tile([P, 2 * P], U32, name=f"q_codes{h}", align_bytes=64))
+            q_scales.append(sb.tile([P, 2 * P], U8, name=f"q_scales{h}", align_bytes=64))
+        nc.vector.tensor_copy(q_bf[0][:].rearrange("p r s j -> p s j r"), q_src[:, :, :, 0:2])
+        nc.scalar.copy(q_bf[1][:].rearrange("p r s j -> p s j r"), q_src[:, :, :, 2:4])
+
+        load_old(0, "slot_d", None)
+        win = [sb.tile([P, 2 * I], F32, name=f"win{r}") for r in range(PACK)]
+        shift = [sb.tile([P, 1], F32, name=f"shift{r}") for r in range(PACK)]
+        pa = [sb.tile([P, I], F32, name=f"pa{r}") for r in range(PACK)]
+        parts = sb.tile([P, PACK, I], F32, name="parts")
+        z = sb.tile([P, PACK], F32, name="z")
+        for h in range(2):
+            nc.vector.quantize_mx(q_codes[h][:].bitcast(FP8X4), q_scales[h][:], q_bf[h][:].rearrange("p r s j -> p (r s j)"))
+            scores = ps.tile([P, 2, I], F32, name=f"scores{h}", tag=f"prod{h}")
+            for u in range(2):
+                cols = slice(u * P, (u + 1) * P)
+                nc.tensor.matmul_mx(
+                    scores[:, u, :], lhsT=q_codes[h][:, cols].bitcast(FP8X4), lhsT_scale=q_scales[h][:, cols],
+                    rhs=k_words[:].bitcast(FP4X4), rhs_scale=k_scales[:], start=True, stop=True,
+                )
+            for u in range(2):
+                r = 2 * h + u
+                nc.vector.tensor_scalar(win[r][:, I:], scores[:, u, :], -0.5, None, ALU.mult, ALU.min, accum_out=shift[r][:])
+                nc.scalar.activation(win[r][:, :I], win[r][:, I:], ACT.Exp, bias=shift[r][:], scale=-1.0)
+                nc.scalar.activation(pa[r][:], win[r][:, :I], ACT.Square)
+
+        load_old(1, "slot_q1", 64)
+        for r in range(PACK):
+            nc.vector.tensor_tensor(parts[:, r, :], win[r][:].indirect(offs2_sb[:]), pa[r][:], ALU.mult)
+            if r < PACK - 1:
+                nc.scalar.activation(parts[:, r, :], parts[:, r, :], ACT.Copy, accum_out=z[:, r : r + 1])
+        r = PACK - 1
+        nc.vector.tensor_scalar(parts[:, r, :], parts[:, r, :], 1.0, None, ALU.mult, ALU.add, accum_out=z[:, r : r + 1])
+
+        g_bf, g_codes, g_scales = [], [], []
+        for j in range(4):
+            g_bf.append(sb.tile([P, P, PACK], BF16, name=f"g_bf{j}", align_bytes=64))
+            g_codes.append(sb.tile([P, P], U32, name=f"g_codes{j}", align_bytes=64))
+            g_scales.append(sb.tile([P, P], U8, name=f"g_scales{j}", align_bytes=64))
+            nc.scalar.copy(
+                g_bf[j][:].rearrange("p (c i) t -> p c t i", i=4),
+                g_raw[:, :, j * P : (j + 1) * P].rearrange("p t (c i) -> p c t i", i=4),
+            )
+
+        def quantize_grows(j):
+            nc.vector.quantize_mx(g_codes[j][:].bitcast(FP8X4), g_scales[j][:], g_bf[j][:].rearrange("p e t -> p (e t)"))
+
+        rz = sb.tile([P, PACK], F32, name="rz")
+        factor = sb.tile([P, PACK], F32, name="factor")
+        quantize_grows(0)
+        nc.vector.reciprocal(rz[:], z[:])
+        nc.vector.tensor_tensor(factor[:], rz[:], qs_sb[:], ALU.mult)
+        quantize_grows(1)
+        w_bf = sb.tile([P, I, PACK], BF16, name="w_bf", tag="late", align_bytes=64)
+        w_codes = sb.tile([P, I], U32, name="w_codes", align_bytes=64)
+        w_scales = sb.tile([P, I], U8, name="w_scales", align_bytes=64)
+        nc.vector.tensor_tensor(
+            w_bf[:].rearrange("p (c i) t -> p c t i", i=4),
+            parts[:].rearrange("p t (c i) -> p c t i", i=4),
+            factor[:].rearrange("p (c t i) -> p c t i", c=1, i=1).to_broadcast([P, I // 4, PACK, 4]),
+            ALU.mult,
+        )
+        quantize_grows(2)
+        nc.vector.quantize_mx(w_codes[:].bitcast(FP8X4), w_scales[:], w_bf[:].rearrange("p i t -> p (i t)"))
+        quantize_grows(3)
+
+        gv = [sb.tile([P, I], F32, name=f"gv{j}", tag=f"slot_gv{j}") for j in range(4)]
+        for j in range(4):
+            bank = ps.tile([P, I], F32, name=f"gv_bank{j}", tag=f"prod{j % 2}")
+            nc.tensor.matmul_mx(
+                bank[:], lhsT=g_codes[j][:].bitcast(FP8X4), lhsT_scale=g_scales[j][:],
+                rhs=w_codes[:].bitcast(FP8X4), rhs_scale=w_scales[:], start=True, stop=True,
+            )
+            nc.scalar.copy(gv[j][:], bank[:])
+
+        fade_col = sb.tile([P, 8], F32, name="fade_col")
+        bank = ps.tile([P, P], F32, name="fade_col_bank", tag="turn0")
+        nc.tensor.transpose(bank[:], fade_rows[:], ident[:])
+        nc.scalar.copy(fade_col[:], bank[:, 0:8])
+        turned = [sb.tile([P, 2, P], F32, name=f"turned{b}") for b in range(8)]
+        for pair in range(4):
+            bank = ps.tile([P, 2, 2, P], F32, name=f"old_bank{pair}", tag=f"turn{(pair + 1) % 2}")
+            for u in range(2):
+                b = 2 * pair + u
+                for j in range(2):
+                    nc.tensor.transpose(bank[:, u, j, :], old_sb[2 + j][:, b * P : (b + 1) * P], ident[:])
+            for u in range(2):
+                b = 2 * pair + u
+                nc.scalar.activation(turned[b][:], bank[:, u, :, :], ACT.Copy, scale=fade_col[:, b : b + 1])
+        faded = {}
+        for h in range(2):
+            for j in range(2):
+                bank = ps.tile([P, 4, P], F32, name=f"faded{j}{h}")
+                faded[j, h] = bank
+                for x in range(4):
+                    nc.tensor.transpose(bank[:, x, :], turned[4 * h + x][:, j, :], ident[:])
+
+        def scatter(j):
+            nc.vector.tensor_copy(gf[j][:].indirect(offs_sb[:]), gv[j][:])
+
+        res = {j: sb.tile([P, T], F32, name=f"res{j}") for j in (2, 3)}
+        res[0] = sb.tile([P, T], F32, name="res0", tag="late", align_bytes=64)
+
+        def finish_gpsimd(j):
+            nc.gpsimd.tensor_tensor(res[j][:], old_sb[j][:], fade_all[:], ALU.mult)
+            for h in range(2):
+                cols = slice(h * BANK, (h + 1) * BANK)
+                nc.gpsimd.tensor_tensor(res[j][:, cols], res[j][:, cols], gf[j][:, cols], ALU.add)
+                nc.sync.dma_start(out[j * P : (j + 1) * P, cols], res[j][:, cols])
+
+        def finish_vector(j):
+            for h in range(2):
+                cols = slice(h * BANK, (h + 1) * BANK)
+                nc.vector.tensor_tensor(res[j][:, cols], faded[j - 2, h][:].rearrange("p x n -> p (x n)"), gf[j][:, cols], ALU.add)
+                nc.sync.dma_start(out[j * P : (j + 1) * P, cols], res[j][:, cols])
+
+        scatter(0)
+        finish_gpsimd(0)
+        scatter(1)
+        scatter(2)
+        finish_vector(2)
+        res[1] = sb.tile([P, T], F32, name="res1", tag="slot_gv0")
+        finish_gpsimd(1)
+        scatter(3)
+        finish_vector(3)

@@ -18,6 +18,7 @@ P = 128
 PACK = 4
 D, E, T, I, Q = 512, 512, 1024, 256, 512
 BANK = 512
+HALF = I // 2
 FLOPS = 2 * D * Q * I + 2 * Q * E * I
 
 
@@ -30,11 +31,10 @@ def tile_attend_blinkedproduct_v_kernel(tc, query, keys_words, keys_scales, qs, 
 
         offs_sb = lists.tile([P, I // 16], U16, name="offs_sb")
         offs2_sb = lists.tile([P, I // 16], U16, name="offs2_sb")
-        words = sb.tile([P, T], U16, name="words", tag="slot_a")
-        kscales = sb.tile([P, T], U8, name="kscales", tag="slot_b")
-        q_raw = sb.tile([P, PACK, Q], F32, name="q_raw", tag="slot_d")
+        words = sb.tile([P, T], U16, name="words")
+        kscales = sb.tile([P, T], U8, name="kscales")
+        q_raw = sb.tile([P, PACK, Q], F32, name="q_raw")
         qs_sb = sb.tile([P, PACK], F32, name="qs_sb")
-        fade8 = sb.tile([P, 8], F32, name="fade8", tag="slot_c")
         fade_rows = sb.tile([P, P], F32, name="fade_rows")
         ident = sb.tile([P, P], F32, name="ident")
         gf = [sb.tile([P, T], F32, name=f"gf{j}") for j in range(4)]
@@ -43,130 +43,135 @@ def tile_attend_blinkedproduct_v_kernel(tc, query, keys_words, keys_scales, qs, 
         nc.gpsimd.memset(kscales[:].bitcast(I32), 0)
         nc.sync.dma_start(offs_sb[:], offs)
         nc.sync.dma_start(words[:].bitcast(I32), keys_words[0].bitcast(I32))
-        nc.sync.dma_start(q_raw[:], query.rearrange("(p j) q -> p j q", j=PACK))
-        nc.scalar.dma_start(fade8[:], fade.rearrange("o (p b) -> p (o b)", b=8))
         for r in range(4):
-            nc.scalar.dma_start(kscales[r:P:32, :].bitcast(I32), keys_scales[0][r:16:4, :].bitcast(I32))
+            nc.sync.dma_start(kscales[r:P:32, :].bitcast(I32), keys_scales[0][r:16:4, :].bitcast(I32))
+        nc.sync.dma_start(q_raw[:], query.rearrange("(p j) q -> p j q", j=PACK))
         make_identity(nc, ident[:])
         nc.gpsimd.memset(fade_rows[:], 0.0)
         nc.scalar.activation(warm[:], ident[:, 0:1], ACT.Exp)
         for j in range(4):
-            nc.vector.memset(gf[j][:], 0.0)
+            (nc.vector if j < 2 else nc.gpsimd).memset(gf[j][:], 0.0)
         nc.sync.dma_start(offs2_sb[:], offs2)
-        nc.gpsimd.dma_start(fade_rows[0:8, :], fade.rearrange("o (b n) -> (o b) n", b=8))
-        nc.gpsimd.dma_start(qs_sb[:], qs.rearrange("(p j) o -> p (j o)", j=PACK))
-
+        g_raw = sb.tile([P, PACK, E], F32, name="g_raw", tag="g_raw")
+        nc.sync.dma_start(g_raw[:], grows.rearrange("(p j) e -> p j e", j=PACK))
+        nc.sync.dma_start(qs_sb[:], qs.rearrange("(p j) o -> p (j o)", j=PACK))
+        nc.sync.dma_start(fade_rows[0:8, :], fade.rearrange("o (b n) -> (o b) n", b=8))
+        old_sb = [sb.tile([P, T], F32, name=f"old{j}") for j in range(4)]
         fade_all = sb.tile([P, T], F32, name="fade_all")
-        fade_nb = fade_all[:].rearrange("p (n b) -> p n b", b=8)
-        for h in range(2):
-            bank = ps.tile([P, 4, P], F32, name=f"fade_bank{h}", tag=f"turn{h}")
-            for b in range(4):
-                col = fade8[:, 4 * h + b : 4 * h + b + 1]
-                nc.tensor.transpose(bank[:, b, :], col.to_broadcast([P, P]), ident[:])
-            nc.scalar.copy(fade_nb[:, :, 4 * h : 4 * h + 4], bank[:].rearrange("p b n -> p n b"))
+        for j in (2, 3, 0):
+            nc.sync.dma_start(old_sb[j][:], old[j * P : (j + 1) * P, :])
+        nc.sync.dma_start(fade_all[:], fade[0].partition_broadcast(P))
+        nc.sync.dma_start(old_sb[1][:], old[P : 2 * P, :])
 
         k_words = sb.tile([P, I], U16, name="k_words", align_bytes=64)
         k_scales = sb.tile([P, I], U8, name="k_scales", align_bytes=64)
         nc.vector.tensor_copy(k_words[:], words[:].indirect(offs_sb[:]))
         nc.vector.tensor_copy(k_scales[:], kscales[:].indirect(offs_sb[:]))
 
-        g_raw = sb.tile([P, PACK, E], F32, name="g_raw", tag="slot_a")
-        nc.sync.dma_start(g_raw[:], grows.rearrange("(p j) e -> p j e", j=PACK))
-        old_sb = {}
-
-        def load_old(j, tag, align):
-            old_sb[j] = sb.tile([P, T], F32, name=f"old{j}", tag=tag, align_bytes=align)
-            nc.sync.dma_start(old_sb[j][:], old[j * P : (j + 1) * P, :])
-
-        load_old(2, "slot_b", None)
-        load_old(3, "slot_c", None)
-
         q_src = q_raw[:].rearrange("p j (s r) -> p s j r", r=PACK)
         q_codes, q_scales, q_bf = [], [], []
         for h in range(2):
-            q_bf.append(sb.tile([P, 2, P, PACK], BF16, name=f"q_bf{h}", tag=f"slot_q{h}", align_bytes=64))
+            q_bf.append(sb.tile([P, 2, P, PACK], BF16, name=f"q_bf{h}", align_bytes=64))
             q_codes.append(sb.tile([P, 2 * P], U32, name=f"q_codes{h}", align_bytes=64))
             q_scales.append(sb.tile([P, 2 * P], U8, name=f"q_scales{h}", align_bytes=64))
         nc.vector.tensor_copy(q_bf[0][:].rearrange("p r s j -> p s j r"), q_src[:, :, :, 0:2])
         nc.scalar.copy(q_bf[1][:].rearrange("p r s j -> p s j r"), q_src[:, :, :, 2:4])
 
-        load_old(0, "slot_d", None)
-        win = [sb.tile([P, 2 * I], F32, name=f"win{r}") for r in range(PACK)]
+        win = [sb.tile([P, I + 8], F32, name=f"win{r}", tag=f"win{r}", align_bytes=64) for r in range(PACK)]
+        for r in range(PACK):
+            nc.gpsimd.memset(win[r][:, I:], 0.0)
         shift = [sb.tile([P, 1], F32, name=f"shift{r}") for r in range(PACK)]
-        pa = [sb.tile([P, I], F32, name=f"pa{r}") for r in range(PACK)]
+        half_shift = [sb.tile([P, 1], F32, name=f"half_shift{r}") for r in range(PACK)]
+        pa = [sb.tile([P, I], F32, name=f"pa{r}", tag=f"pa{r}", align_bytes=64) for r in range(PACK)]
         parts = sb.tile([P, PACK, I], F32, name="parts")
         z = sb.tile([P, PACK], F32, name="z")
-        for h in range(2):
-            nc.vector.quantize_mx(q_codes[h][:].bitcast(FP8X4), q_scales[h][:], q_bf[h][:].rearrange("p r s j -> p (r s j)"))
-            scores = ps.tile([P, 2, I], F32, name=f"scores{h}", tag=f"prod{h}")
-            for u in range(2):
-                cols = slice(u * P, (u + 1) * P)
-                nc.tensor.matmul_mx(
-                    scores[:, u, :], lhsT=q_codes[h][:, cols].bitcast(FP8X4), lhsT_scale=q_scales[h][:, cols],
-                    rhs=k_words[:].bitcast(FP4X4), rhs_scale=k_scales[:], start=True, stop=True,
-                )
-            for u in range(2):
-                r = 2 * h + u
-                nc.vector.tensor_scalar(win[r][:, I:], scores[:, u, :], -0.5, None, ALU.mult, ALU.min, accum_out=shift[r][:])
-                nc.scalar.activation(win[r][:, :I], win[r][:, I:], ACT.Exp, bias=shift[r][:], scale=-1.0)
-                nc.scalar.activation(pa[r][:], win[r][:, :I], ACT.Square)
+        scores = [ps.tile([P, I], F32, name=f"scores{r}", tag=f"prod{r}") for r in range(PACK)]
+        for r in range(PACK):
+            h, u = divmod(r, 2)
+            cols = slice(u * P, (u + 1) * P)
+            nc.vector.quantize_mx(q_codes[h][:, cols].bitcast(FP8X4), q_scales[h][:, cols], q_bf[h][:, u].rearrange("p s j -> p (s j)"))
+            nc.tensor.matmul_mx(
+                scores[r][:], lhsT=q_codes[h][:, cols].bitcast(FP8X4), lhsT_scale=q_scales[h][:, cols],
+                rhs=k_words[:].bitcast(FP4X4), rhs_scale=k_scales[:], start=True, stop=True,
+            )
+        for r in range(PACK):
+            nc.vector.tensor_reduce(shift[r][:], scores[r][:], mybir.AxisListType.X, ALU.max, negate=True)
+            nc.scalar.activation(half_shift[r][:], shift[r][:], ACT.Copy, scale=0.5)
+            nc.scalar.activation(pa[r][:], scores[r][:], ACT.Exp, bias=shift[r][:])
+            nc.scalar.activation(win[r][:, :I], scores[r][:], ACT.Exp, bias=half_shift[r][:], scale=0.5)
 
-        load_old(1, "slot_q1", 64)
         for r in range(PACK):
             nc.vector.tensor_tensor(parts[:, r, :], win[r][:].indirect(offs2_sb[:]), pa[r][:], ALU.mult)
-            if r < PACK - 1:
-                nc.scalar.activation(parts[:, r, :], parts[:, r, :], ACT.Copy, accum_out=z[:, r : r + 1])
         r = PACK - 1
         nc.vector.tensor_scalar(parts[:, r, :], parts[:, r, :], 1.0, None, ALU.mult, ALU.add, accum_out=z[:, r : r + 1])
 
-        g_bf, g_codes, g_scales = [], [], []
-        for j in range(4):
-            g_bf.append(sb.tile([P, P, PACK], BF16, name=f"g_bf{j}", align_bytes=64))
-            g_codes.append(sb.tile([P, P], U32, name=f"g_codes{j}", align_bytes=64))
-            g_scales.append(sb.tile([P, P], U8, name=f"g_scales{j}", align_bytes=64))
+        g_bf = [sb.tile([P, P, PACK], BF16, name=f"g_bf{j}", tag=tag, align_bytes=64) for j, tag in enumerate(("pa2", "pa3", "win2", "win3"))]
+        g_codes = [sb.tile([P, P], U32, name=f"g_codes{j}", align_bytes=64) for j in range(4)]
+        g_scales = [sb.tile([P, P], U8, name=f"g_scales{j}", align_bytes=64) for j in range(4)]
+
+        def weave_grows(j):
             nc.scalar.copy(
                 g_bf[j][:].rearrange("p (c i) t -> p c t i", i=4),
                 g_raw[:, :, j * P : (j + 1) * P].rearrange("p t (c i) -> p c t i", i=4),
             )
+
+        def row_sum(r):
+            nc.scalar.activation(parts[:, r, :], parts[:, r, :], ACT.Copy, accum_out=z[:, r : r + 1])
+
+        for r in range(PACK - 1):
+            row_sum(r)
+        for j in range(4):
+            weave_grows(j)
 
         def quantize_grows(j):
             nc.vector.quantize_mx(g_codes[j][:].bitcast(FP8X4), g_scales[j][:], g_bf[j][:].rearrange("p e t -> p (e t)"))
 
         rz = sb.tile([P, PACK], F32, name="rz")
         factor = sb.tile([P, PACK], F32, name="factor")
-        quantize_grows(0)
         nc.vector.reciprocal(rz[:], z[:])
+        quantize_grows(0)
         nc.vector.tensor_tensor(factor[:], rz[:], qs_sb[:], ALU.mult)
-        quantize_grows(1)
-        w_bf = sb.tile([P, I, PACK], BF16, name="w_bf", tag="late", align_bytes=64)
+        w_bf = [sb.tile([P, HALF, PACK], BF16, name=f"w_bf{h}", tag=f"late{h}", align_bytes=64) for h in range(2)]
         w_codes = sb.tile([P, I], U32, name="w_codes", align_bytes=64)
         w_scales = sb.tile([P, I], U8, name="w_scales", align_bytes=64)
-        nc.vector.tensor_tensor(
-            w_bf[:].rearrange("p (c i) t -> p c t i", i=4),
-            parts[:].rearrange("p t (c i) -> p c t i", i=4),
-            factor[:].rearrange("p (c t i) -> p c t i", c=1, i=1).to_broadcast([P, I // 4, PACK, 4]),
-            ALU.mult,
-        )
-        quantize_grows(2)
-        nc.vector.quantize_mx(w_codes[:].bitcast(FP8X4), w_scales[:], w_bf[:].rearrange("p i t -> p (i t)"))
-        quantize_grows(3)
+        halves = [slice(h * HALF, (h + 1) * HALF) for h in range(2)]
+        for h in range(2):
+            nc.vector.tensor_tensor(
+                w_bf[h][:].rearrange("p (c i) t -> p c t i", i=4),
+                parts[:, :, halves[h]].rearrange("p t (c i) -> p c t i", i=4),
+                factor[:].rearrange("p (c t i) -> p c t i", c=1, i=1).to_broadcast([P, HALF // 4, PACK, 4]),
+                ALU.mult,
+            )
+        for h in range(2):
+            nc.vector.quantize_mx(w_codes[:, halves[h]].bitcast(FP8X4), w_scales[:, halves[h]], w_bf[h][:].rearrange("p i t -> p (i t)"))
+        quantize_grows(1)
 
         gv = [sb.tile([P, I], F32, name=f"gv{j}", tag=f"slot_gv{j}") for j in range(4)]
-        for j in range(4):
-            bank = ps.tile([P, I], F32, name=f"gv_bank{j}", tag=f"prod{j % 2}")
+
+        def gradient(j, slots, tag):
+            bank = ps.tile([P, slots.stop - slots.start], F32, name=f"gv_bank{j}_{slots.start}", tag=tag)
             nc.tensor.matmul_mx(
                 bank[:], lhsT=g_codes[j][:].bitcast(FP8X4), lhsT_scale=g_scales[j][:],
-                rhs=w_codes[:].bitcast(FP8X4), rhs_scale=w_scales[:], start=True, stop=True,
+                rhs=w_codes[:, slots].bitcast(FP8X4), rhs_scale=w_scales[:, slots], start=True, stop=True,
             )
-            nc.scalar.copy(gv[j][:], bank[:])
+            nc.scalar.copy(gv[j][:, slots], bank[:])
 
-        fade_col = sb.tile([P, 8], F32, name="fade_col")
-        bank = ps.tile([P, P], F32, name="fade_col_bank", tag="turn0")
+        for h in range(2):
+            gradient(0, halves[h], f"prod{h}")
+        nc.vector.tensor_copy(gf[0][:].indirect(offs_sb[:, 0:8]), gv[0][:, halves[0]])
+        quantize_grows(2)
+        quantize_grows(3)
+        nc.vector.tensor_copy(gf[0][:].indirect(offs_sb[:, 8:16]), gv[0][:, halves[1]])
+        for j in range(1, 4):
+            gradient(j, slice(0, I), f"prod{j % 2}")
+
+        fade_col = sb.tile([P, 8], F32, name="fade_col", tag="g_raw")
+        bank = ps.tile([P, P], F32, name="fade_col_bank", tag="prod2")
         nc.tensor.transpose(bank[:], fade_rows[:], ident[:])
         nc.scalar.copy(fade_col[:], bank[:, 0:8])
         turned = [sb.tile([P, 2, P], F32, name=f"turned{b}") for b in range(8)]
         for pair in range(4):
-            bank = ps.tile([P, 2, 2, P], F32, name=f"old_bank{pair}", tag=f"turn{(pair + 1) % 2}")
+            bank = ps.tile([P, 2, 2, P], F32, name=f"old_bank{pair}", tag=f"prod{3 - pair % 2}")
             for u in range(2):
                 b = 2 * pair + u
                 for j in range(2):
@@ -186,12 +191,12 @@ def tile_attend_blinkedproduct_v_kernel(tc, query, keys_words, keys_scales, qs, 
             nc.vector.tensor_copy(gf[j][:].indirect(offs_sb[:]), gv[j][:])
 
         res = {j: sb.tile([P, T], F32, name=f"res{j}") for j in (2, 3)}
-        res[0] = sb.tile([P, T], F32, name="res0", tag="late", align_bytes=64)
+        res[0] = sb.tile([P, T], F32, name="res0", tag="late1", align_bytes=64)
 
-        def finish_gpsimd(j):
+        def finish_gpsimd(j, pieces):
             nc.gpsimd.tensor_tensor(res[j][:], old_sb[j][:], fade_all[:], ALU.mult)
-            for h in range(2):
-                cols = slice(h * BANK, (h + 1) * BANK)
+            for h in range(pieces):
+                cols = slice(h * T // pieces, (h + 1) * T // pieces)
                 nc.gpsimd.tensor_tensor(res[j][:, cols], res[j][:, cols], gf[j][:, cols], ALU.add)
                 nc.sync.dma_start(out[j * P : (j + 1) * P, cols], res[j][:, cols])
 
@@ -201,12 +206,11 @@ def tile_attend_blinkedproduct_v_kernel(tc, query, keys_words, keys_scales, qs, 
                 nc.vector.tensor_tensor(res[j][:, cols], faded[j - 2, h][:].rearrange("p x n -> p (x n)"), gf[j][:, cols], ALU.add)
                 nc.sync.dma_start(out[j * P : (j + 1) * P, cols], res[j][:, cols])
 
-        scatter(0)
-        finish_gpsimd(0)
+        finish_gpsimd(0, 1)
         scatter(1)
         scatter(2)
         finish_vector(2)
         res[1] = sb.tile([P, T], F32, name="res1", tag="slot_gv0")
-        finish_gpsimd(1)
+        finish_gpsimd(1, 2)
         scatter(3)
         finish_vector(3)

@@ -131,7 +131,7 @@ def tile_attend_blinkedproduct_v_kernel(tc, query, keys_words, keys_scales, qs, 
         nc.vector.reciprocal(rz[:], z[:])
         quantize_grows(0)
         nc.vector.tensor_tensor(factor[:], rz[:], qs_sb[:], ALU.mult)
-        w_bf = [sb.tile([P, HALF, PACK], BF16, name=f"w_bf{h}", tag=f"late{h}", align_bytes=64) for h in range(2)]
+        w_bf = [sb.tile([P, HALF, PACK], BF16, name=f"w_bf{h}", align_bytes=64) for h in range(2)]
         w_codes = sb.tile([P, I], U32, name="w_codes", align_bytes=64)
         w_scales = sb.tile([P, I], U8, name="w_scales", align_bytes=64)
         halves = [slice(h * HALF, (h + 1) * HALF) for h in range(2)]
@@ -144,9 +144,10 @@ def tile_attend_blinkedproduct_v_kernel(tc, query, keys_words, keys_scales, qs, 
             )
         for h in range(2):
             nc.vector.quantize_mx(w_codes[:, halves[h]].bitcast(FP8X4), w_scales[:, halves[h]], w_bf[h][:].rearrange("p i t -> p (i t)"))
-        quantize_grows(1)
+        for j in range(1, 4):
+            quantize_grows(j)
 
-        gv = [sb.tile([P, I], F32, name=f"gv{j}", tag=f"slot_gv{j}") for j in range(4)]
+        gv = [sb.tile([P, I], F32, name=f"gv{j}", tag=f"slot_gv{j}") for j in range(3)]
 
         def gradient(j, slots, tag):
             bank = ps.tile([P, slots.stop - slots.start], F32, name=f"gv_bank{j}_{slots.start}", tag=tag)
@@ -158,18 +159,14 @@ def tile_attend_blinkedproduct_v_kernel(tc, query, keys_words, keys_scales, qs, 
 
         for h in range(2):
             gradient(0, halves[h], f"prod{h}")
-        nc.vector.tensor_copy(gf[0][:].indirect(offs_sb[:, 0:8]), gv[0][:, halves[0]])
-        quantize_grows(2)
-        quantize_grows(3)
-        nc.vector.tensor_copy(gf[0][:].indirect(offs_sb[:, 8:16]), gv[0][:, halves[1]])
-        for j in range(1, 4):
+        for j in range(1, 3):
             gradient(j, slice(0, I), f"prod{j % 2}")
 
         fade_col = sb.tile([P, 8], F32, name="fade_col", tag="g_raw")
         bank = ps.tile([P, P], F32, name="fade_col_bank", tag="prod2")
         nc.tensor.transpose(bank[:], fade_rows[:], ident[:])
         nc.scalar.copy(fade_col[:], bank[:, 0:8])
-        turned = [sb.tile([P, 2, P], F32, name=f"turned{b}") for b in range(8)]
+        turned = sb.tile([P, 8, 2, P], F32, name="turned", tag="turned")
         for pair in range(4):
             bank = ps.tile([P, 2, 2, P], F32, name=f"old_bank{pair}", tag=f"prod{3 - pair % 2}")
             for u in range(2):
@@ -178,27 +175,30 @@ def tile_attend_blinkedproduct_v_kernel(tc, query, keys_words, keys_scales, qs, 
                     nc.tensor.transpose(bank[:, u, j, :], old_sb[2 + j][:, b * P : (b + 1) * P], ident[:])
             for u in range(2):
                 b = 2 * pair + u
-                nc.scalar.activation(turned[b][:], bank[:, u, :, :], ACT.Copy, scale=fade_col[:, b : b + 1])
+                nc.scalar.activation(turned[:, b], bank[:, u, :, :], ACT.Copy, scale=fade_col[:, b : b + 1])
         faded = {}
         for h in range(2):
             for j in range(2):
                 bank = ps.tile([P, 4, P], F32, name=f"faded{j}{h}")
                 faded[j, h] = bank
                 for x in range(4):
-                    nc.tensor.transpose(bank[:, x, :], turned[4 * h + x][:, j, :], ident[:])
+                    nc.tensor.transpose(bank[:, x, :], turned[:, 4 * h + x, j, :], ident[:])
+
+        gv.append(sb.tile([P, I], F32, name="gv3", tag="turned"))
+        gradient(3, slice(0, I), "prod1")
 
         def scatter(j):
             nc.vector.tensor_copy(gf[j][:].indirect(offs_sb[:]), gv[j][:])
 
         res = {j: sb.tile([P, T], F32, name=f"res{j}") for j in (2, 3)}
-        res[0] = sb.tile([P, T], F32, name="res0", tag="late1", align_bytes=64)
+        res[0] = sb.tile([P, T], F32, name="res0", tag="win3", align_bytes=64)
 
-        def finish_gpsimd(j, pieces):
+        def finish_gpsimd(j, pieces, queue):
             nc.gpsimd.tensor_tensor(res[j][:], old_sb[j][:], fade_all[:], ALU.mult)
             for h in range(pieces):
                 cols = slice(h * T // pieces, (h + 1) * T // pieces)
                 nc.gpsimd.tensor_tensor(res[j][:, cols], res[j][:, cols], gf[j][:, cols], ALU.add)
-                nc.sync.dma_start(out[j * P : (j + 1) * P, cols], res[j][:, cols])
+                queue.dma_start(out[j * P : (j + 1) * P, cols], res[j][:, cols])
 
         def finish_vector(j):
             for h in range(2):
@@ -206,11 +206,12 @@ def tile_attend_blinkedproduct_v_kernel(tc, query, keys_words, keys_scales, qs, 
                 nc.vector.tensor_tensor(res[j][:, cols], faded[j - 2, h][:].rearrange("p x n -> p (x n)"), gf[j][:, cols], ALU.add)
                 nc.sync.dma_start(out[j * P : (j + 1) * P, cols], res[j][:, cols])
 
-        finish_gpsimd(0, 1)
+        scatter(0)
+        finish_gpsimd(0, 1, nc.sync)
         scatter(1)
         scatter(2)
         finish_vector(2)
         res[1] = sb.tile([P, T], F32, name="res1", tag="slot_gv0")
-        finish_gpsimd(1, 2)
+        finish_gpsimd(1, 2, nc.scalar)
         scatter(3)
         finish_vector(3)

@@ -42,7 +42,7 @@ def tile_attend_blinkedproduct_v_kernel(tc, query, keys_words, keys_scales, qs, 
 
         nc.gpsimd.memset(kscales[:].bitcast(I32), 0)
         nc.sync.dma_start(offs_sb[:], offs)
-        nc.sync.dma_start(words[:].bitcast(I32), keys_words[0].bitcast(I32))
+        nc.scalar.dma_start(words[:].bitcast(I32), keys_words[0].bitcast(I32))
         for r in range(4):
             nc.sync.dma_start(kscales[r:P:32, :].bitcast(I32), keys_scales[0][r:16:4, :].bitcast(I32))
         nc.sync.dma_start(q_raw[:], query.rearrange("(p j) q -> p j q", j=PACK))
@@ -52,16 +52,15 @@ def tile_attend_blinkedproduct_v_kernel(tc, query, keys_words, keys_scales, qs, 
         for j in range(4):
             (nc.vector if j < 2 else nc.gpsimd).memset(gf[j][:], 0.0)
         nc.sync.dma_start(offs2_sb[:], offs2)
-        g_raw = sb.tile([P, PACK, E], F32, name="g_raw", tag="g_raw")
+        g_raw = sb.tile([P, PACK, E], F32, name="g_raw", tag="turned")
         nc.sync.dma_start(g_raw[:], grows.rearrange("(p j) e -> p j e", j=PACK))
         nc.sync.dma_start(qs_sb[:], qs.rearrange("(p j) o -> p (j o)", j=PACK))
         nc.sync.dma_start(fade_rows[0:8, :], fade.rearrange("o (b n) -> (o b) n", b=8))
         old_sb = [sb.tile([P, T], F32, name=f"old{j}") for j in range(4)]
         fade_all = sb.tile([P, T], F32, name="fade_all")
-        for j in (2, 3, 0):
+        for j in (2, 3, 1, 0):
             nc.sync.dma_start(old_sb[j][:], old[j * P : (j + 1) * P, :])
         nc.sync.dma_start(fade_all[:], fade[0].partition_broadcast(P))
-        nc.sync.dma_start(old_sb[1][:], old[P : 2 * P, :])
 
         k_words = sb.tile([P, I], U16, name="k_words", align_bytes=64)
         k_scales = sb.tile([P, I], U8, name="k_scales", align_bytes=64)
@@ -147,7 +146,8 @@ def tile_attend_blinkedproduct_v_kernel(tc, query, keys_words, keys_scales, qs, 
         for j in range(1, 4):
             quantize_grows(j)
 
-        gv = [sb.tile([P, I], F32, name=f"gv{j}", tag=f"slot_gv{j}") for j in range(3)]
+        gv_tiles = [sb.tile([P, I], F32, name=f"gv{j}") for j in range(3)]
+        gv = [tile[:] for tile in gv_tiles]
 
         def gradient(j, slots, tag):
             bank = ps.tile([P, slots.stop - slots.start], F32, name=f"gv_bank{j}_{slots.start}", tag=tag)
@@ -162,13 +162,13 @@ def tile_attend_blinkedproduct_v_kernel(tc, query, keys_words, keys_scales, qs, 
         for j in range(1, 3):
             gradient(j, slice(0, I), f"prod{j % 2}")
 
-        fade_col = sb.tile([P, 8], F32, name="fade_col", tag="g_raw")
-        bank = ps.tile([P, P], F32, name="fade_col_bank", tag="prod2")
+        fade_col = sb.tile([P, 8], F32, name="fade_col")
+        bank = ps.tile([P, P], F32, name="fade_col_bank", tag="back00")
         nc.tensor.transpose(bank[:], fade_rows[:], ident[:])
         nc.scalar.copy(fade_col[:], bank[:, 0:8])
         turned = sb.tile([P, 8, 2, P], F32, name="turned", tag="turned")
-        for pair in range(4):
-            bank = ps.tile([P, 2, 2, P], F32, name=f"old_bank{pair}", tag=f"prod{3 - pair % 2}")
+        for pair, tag in enumerate(("prod2", "prod3", "back01", "back11")):
+            bank = ps.tile([P, 2, 2, P], F32, name=f"old_bank{pair}", tag=tag)
             for u in range(2):
                 b = 2 * pair + u
                 for j in range(2):
@@ -179,39 +179,52 @@ def tile_attend_blinkedproduct_v_kernel(tc, query, keys_words, keys_scales, qs, 
         faded = {}
         for h in range(2):
             for j in range(2):
-                bank = ps.tile([P, 4, P], F32, name=f"faded{j}{h}")
+                bank = ps.tile([P, 4, P], F32, name=f"faded{j}{h}", tag=f"back{j}{h}")
                 faded[j, h] = bank
                 for x in range(4):
                     nc.tensor.transpose(bank[:, x, :], turned[:, 4 * h + x, j, :], ident[:])
 
-        gv.append(sb.tile([P, I], F32, name="gv3", tag="turned"))
-        gradient(3, slice(0, I), "prod1")
+        turned1 = sb.tile([P, 4, P], F32, name="turned1")
+        faded1 = sb.tile([P, BANK], F32, name="faded1", tag="faded1")
+        bank = ps.tile([P, 4, P], F32, name="old1_bank", tag="prod2")
+        for x in range(4):
+            nc.tensor.transpose(bank[:, x, :], old_sb[1][:, BANK + x * P : BANK + (x + 1) * P], ident[:])
+        for x in range(4):
+            nc.scalar.activation(turned1[:, x, :], bank[:, x, :], ACT.Copy, scale=fade_col[:, 4 + x : 5 + x])
+        bank = ps.tile([P, 4, P], F32, name="faded1_bank", tag="prod3")
+        for x in range(4):
+            nc.tensor.transpose(bank[:, x, :], turned1[:, x, :], ident[:])
+        nc.scalar.copy(faded1[:], bank[:].rearrange("p x n -> p (x n)"))
 
         def scatter(j):
-            nc.vector.tensor_copy(gf[j][:].indirect(offs_sb[:]), gv[j][:])
+            nc.vector.tensor_copy(gf[j][:].indirect(offs_sb[:]), gv[j])
 
-        res = {j: sb.tile([P, T], F32, name=f"res{j}") for j in (2, 3)}
-        res[0] = sb.tile([P, T], F32, name="res0", tag="win3", align_bytes=64)
-
-        def finish_gpsimd(j, pieces, queue):
-            nc.gpsimd.tensor_tensor(res[j][:], old_sb[j][:], fade_all[:], ALU.mult)
-            for h in range(pieces):
-                cols = slice(h * T // pieces, (h + 1) * T // pieces)
-                nc.gpsimd.tensor_tensor(res[j][:, cols], res[j][:, cols], gf[j][:, cols], ALU.add)
-                queue.dma_start(out[j * P : (j + 1) * P, cols], res[j][:, cols])
-
-        def finish_vector(j):
+        def finish_vector(j, res):
             for h in range(2):
                 cols = slice(h * BANK, (h + 1) * BANK)
-                nc.vector.tensor_tensor(res[j][:, cols], faded[j - 2, h][:].rearrange("p x n -> p (x n)"), gf[j][:, cols], ALU.add)
-                nc.sync.dma_start(out[j * P : (j + 1) * P, cols], res[j][:, cols])
+                nc.vector.tensor_tensor(res[:, cols], faded[j - 2, h][:].rearrange("p x n -> p (x n)"), gf[j][:, cols], ALU.add)
+                nc.sync.dma_start(out[j * P : (j + 1) * P, cols], res[:, cols])
 
+        faded0 = sb.tile([P, T], F32, name="faded0", tag="win3", align_bytes=64)
+        res0 = sb.tile([P, T], F32, name="res0")
+        nc.gpsimd.tensor_tensor(faded0[:], old_sb[0][:], fade_all[:], ALU.mult)
         scatter(0)
-        finish_gpsimd(0, 1, nc.sync)
+        nc.gpsimd.tensor_tensor(res0[:], faded0[:], gf[0][:], ALU.add)
+        nc.sync.dma_start(out[0:P, :], res0[:])
+        late = sb.tile([P, T + I + BANK], F32, name="late", tag="win3", align_bytes=64)
+        res2, faded1_low = late[:, :T], late[:, T + I :]
+        gv.append(late[:, T : T + I])
+        gradient(3, slice(0, I), "prod1")
         scatter(1)
         scatter(2)
-        finish_vector(2)
-        res[1] = sb.tile([P, T], F32, name="res1", tag="slot_gv0")
-        finish_gpsimd(1, 2, nc.scalar)
+        finish_vector(2, res2)
+        nc.gpsimd.tensor_tensor(faded1_low, old_sb[1][:, :BANK], fade_all[:, :BANK], ALU.mult)
+        res1_high = sb.tile([P, BANK], F32, name="res1_high")
+        nc.gpsimd.tensor_tensor(res1_high[:], faded1[:], gf[1][:, BANK:], ALU.add)
+        nc.scalar.dma_start(out[P : 2 * P, BANK:], res1_high[:])
+        res1_low = sb.tile([P, BANK], F32, name="res1_low", tag="faded1")
+        nc.gpsimd.tensor_tensor(res1_low[:], faded1_low, gf[1][:, :BANK], ALU.add)
+        nc.scalar.dma_start(out[P : 2 * P, :BANK], res1_low[:])
         scatter(3)
-        finish_vector(3)
+        res3 = sb.tile([P, T], F32, name="res3")
+        finish_vector(3, res3[:])

from contextlib import ExitStack

import concourse.mybir as mybir
from concourse.masks import make_identity

F32 = mybir.dt.float32
BF16 = mybir.dt.bfloat16
I32 = mybir.dt.int32
U32 = mybir.dt.uint32
U16 = mybir.dt.uint16
U8 = mybir.dt.uint8
FP8X4 = mybir.dt.float8_e4m3fn_x4
FP4X4 = mybir.dt.float4_e2m1fn_x4
ALU = mybir.AluOpType
ACT = mybir.ActivationFunctionType

P = 128
PACK = 4
D, E, T, I, Q = 512, 512, 1024, 256, 512
BANK = 512
HALF = I // 2
FLOPS = 2 * D * Q * I + 2 * Q * E * I


def tile_attend_blinkedproduct_v_kernel(tc, query, keys_words, keys_scales, qs, grows, old, fade, offs2, offs, out):
    nc = tc.nc
    with ExitStack() as ctx:
        lists = ctx.enter_context(tc.tile_pool(name="lists", bufs=1))
        sb = ctx.enter_context(tc.tile_pool(name="sb", bufs=1))
        ps = ctx.enter_context(tc.psum_pool(name="ps", bufs=1))

        offs_sb = lists.tile([P, I // 16], U16, name="offs_sb")
        offs2_sb = lists.tile([P, I // 16], U16, name="offs2_sb")
        words = sb.tile([P, T], U16, name="words")
        kscales = sb.tile([P, T], U8, name="kscales")
        q_raw = sb.tile([P, PACK, Q], F32, name="q_raw")
        qs_sb = sb.tile([P, PACK], F32, name="qs_sb")
        fade_rows = sb.tile([P, P], F32, name="fade_rows")
        ident = sb.tile([P, P], F32, name="ident")
        gf = [sb.tile([P, T], F32, name=f"gf{j}") for j in range(4)]
        warm = sb.tile([P, 1], F32, name="warm")

        nc.gpsimd.memset(kscales[:].bitcast(I32), 0)
        nc.sync.dma_start(offs_sb[:], offs)
        nc.scalar.dma_start(words[:].bitcast(I32), keys_words[0].bitcast(I32))
        for r in range(4):
            nc.sync.dma_start(kscales[r:P:32, :].bitcast(I32), keys_scales[0][r:16:4, :].bitcast(I32))
        nc.sync.dma_start(q_raw[:], query.rearrange("(p j) q -> p j q", j=PACK))
        make_identity(nc, ident[:])
        nc.gpsimd.memset(fade_rows[:], 0.0)
        nc.scalar.activation(warm[:], ident[:, 0:1], ACT.Exp)
        for j in range(4):
            (nc.vector if j < 2 else nc.gpsimd).memset(gf[j][:], 0.0)
        nc.sync.dma_start(offs2_sb[:], offs2)
        g_raw = sb.tile([P, PACK, E], F32, name="g_raw", tag="turned")
        nc.sync.dma_start(g_raw[:], grows.rearrange("(p j) e -> p j e", j=PACK))
        nc.sync.dma_start(qs_sb[:], qs.rearrange("(p j) o -> p (j o)", j=PACK))
        nc.sync.dma_start(fade_rows[0:8, :], fade.rearrange("o (b n) -> (o b) n", b=8))
        old_sb = [sb.tile([P, T], F32, name=f"old{j}") for j in range(4)]
        fade_all = sb.tile([P, T], F32, name="fade_all")
        for j in (2, 3, 1, 0):
            nc.sync.dma_start(old_sb[j][:], old[j * P : (j + 1) * P, :])
        nc.sync.dma_start(fade_all[:], fade[0].partition_broadcast(P))

        k_words = sb.tile([P, I], U16, name="k_words", align_bytes=64)
        k_scales = sb.tile([P, I], U8, name="k_scales", align_bytes=64)
        nc.vector.tensor_copy(k_words[:], words[:].indirect(offs_sb[:]))
        nc.vector.tensor_copy(k_scales[:], kscales[:].indirect(offs_sb[:]))

        q_src = q_raw[:].rearrange("p j (s r) -> p s j r", r=PACK)
        q_codes, q_scales, q_bf = [], [], []
        for h in range(2):
            q_bf.append(sb.tile([P, 2, P, PACK], BF16, name=f"q_bf{h}", align_bytes=64))
            q_codes.append(sb.tile([P, 2 * P], U32, name=f"q_codes{h}", align_bytes=64))
            q_scales.append(sb.tile([P, 2 * P], U8, name=f"q_scales{h}", align_bytes=64))
        nc.vector.tensor_copy(q_bf[0][:].rearrange("p r s j -> p s j r"), q_src[:, :, :, 0:2])
        nc.scalar.copy(q_bf[1][:].rearrange("p r s j -> p s j r"), q_src[:, :, :, 2:4])

        win = [sb.tile([P, I + 8], F32, name=f"win{r}", tag=f"win{r}", align_bytes=64) for r in range(PACK)]
        for r in range(PACK):
            nc.gpsimd.memset(win[r][:, I:], 0.0)
        shift = [sb.tile([P, 1], F32, name=f"shift{r}") for r in range(PACK)]
        half_shift = [sb.tile([P, 1], F32, name=f"half_shift{r}") for r in range(PACK)]
        pa = [sb.tile([P, I], F32, name=f"pa{r}", tag=f"pa{r}", align_bytes=64) for r in range(PACK)]
        parts = sb.tile([P, PACK, I], F32, name="parts")
        z = sb.tile([P, PACK], F32, name="z")
        scores = [ps.tile([P, I], F32, name=f"scores{r}", tag=f"prod{r}") for r in range(PACK)]
        for r in range(PACK):
            h, u = divmod(r, 2)
            cols = slice(u * P, (u + 1) * P)
            nc.vector.quantize_mx(q_codes[h][:, cols].bitcast(FP8X4), q_scales[h][:, cols], q_bf[h][:, u].rearrange("p s j -> p (s j)"))
            nc.tensor.matmul_mx(
                scores[r][:], lhsT=q_codes[h][:, cols].bitcast(FP8X4), lhsT_scale=q_scales[h][:, cols],
                rhs=k_words[:].bitcast(FP4X4), rhs_scale=k_scales[:], start=True, stop=True,
            )
        for r in range(PACK):
            nc.vector.tensor_reduce(shift[r][:], scores[r][:], mybir.AxisListType.X, ALU.max, negate=True)
            nc.scalar.activation(half_shift[r][:], shift[r][:], ACT.Copy, scale=0.5)
            nc.scalar.activation(pa[r][:], scores[r][:], ACT.Exp, bias=shift[r][:])
            nc.scalar.activation(win[r][:, :I], scores[r][:], ACT.Exp, bias=half_shift[r][:], scale=0.5)

        for r in range(PACK):
            nc.vector.tensor_tensor(parts[:, r, :], win[r][:].indirect(offs2_sb[:]), pa[r][:], ALU.mult)
        r = PACK - 1
        nc.vector.tensor_scalar(parts[:, r, :], parts[:, r, :], 1.0, None, ALU.mult, ALU.add, accum_out=z[:, r : r + 1])

        g_bf = [sb.tile([P, P, PACK], BF16, name=f"g_bf{j}", tag=tag, align_bytes=64) for j, tag in enumerate(("pa2", "pa3", "win2", "win3"))]
        g_codes = [sb.tile([P, P], U32, name=f"g_codes{j}", align_bytes=64) for j in range(4)]
        g_scales = [sb.tile([P, P], U8, name=f"g_scales{j}", align_bytes=64) for j in range(4)]

        def weave_grows(j):
            nc.scalar.copy(
                g_bf[j][:].rearrange("p (c i) t -> p c t i", i=4),
                g_raw[:, :, j * P : (j + 1) * P].rearrange("p t (c i) -> p c t i", i=4),
            )

        def row_sum(r):
            nc.scalar.activation(parts[:, r, :], parts[:, r, :], ACT.Copy, accum_out=z[:, r : r + 1])

        for r in range(PACK - 1):
            row_sum(r)
        for j in range(4):
            weave_grows(j)

        def quantize_grows(j):
            nc.vector.quantize_mx(g_codes[j][:].bitcast(FP8X4), g_scales[j][:], g_bf[j][:].rearrange("p e t -> p (e t)"))

        rz = sb.tile([P, PACK], F32, name="rz")
        factor = sb.tile([P, PACK], F32, name="factor")
        nc.vector.reciprocal(rz[:], z[:])
        quantize_grows(0)
        nc.vector.tensor_tensor(factor[:], rz[:], qs_sb[:], ALU.mult)
        w_bf = [sb.tile([P, HALF, PACK], BF16, name=f"w_bf{h}", align_bytes=64) for h in range(2)]
        w_codes = sb.tile([P, I], U32, name="w_codes", align_bytes=64)
        w_scales = sb.tile([P, I], U8, name="w_scales", align_bytes=64)
        halves = [slice(h * HALF, (h + 1) * HALF) for h in range(2)]
        for h in range(2):
            nc.vector.tensor_tensor(
                w_bf[h][:].rearrange("p (c i) t -> p c t i", i=4),
                parts[:, :, halves[h]].rearrange("p t (c i) -> p c t i", i=4),
                factor[:].rearrange("p (c t i) -> p c t i", c=1, i=1).to_broadcast([P, HALF // 4, PACK, 4]),
                ALU.mult,
            )
        for h in range(2):
            nc.vector.quantize_mx(w_codes[:, halves[h]].bitcast(FP8X4), w_scales[:, halves[h]], w_bf[h][:].rearrange("p i t -> p (i t)"))
        for j in range(1, 4):
            quantize_grows(j)

        gv_tiles = [sb.tile([P, I], F32, name=f"gv{j}") for j in range(3)]
        gv = [tile[:] for tile in gv_tiles]

        def gradient(j, slots, tag):
            bank = ps.tile([P, slots.stop - slots.start], F32, name=f"gv_bank{j}_{slots.start}", tag=tag)
            nc.tensor.matmul_mx(
                bank[:], lhsT=g_codes[j][:].bitcast(FP8X4), lhsT_scale=g_scales[j][:],
                rhs=w_codes[:, slots].bitcast(FP8X4), rhs_scale=w_scales[:, slots], start=True, stop=True,
            )
            nc.scalar.copy(gv[j][:, slots], bank[:])

        for h in range(2):
            gradient(0, halves[h], f"prod{h}")
        for j in range(1, 3):
            gradient(j, slice(0, I), f"prod{j % 2}")

        fade_col = sb.tile([P, 8], F32, name="fade_col")
        bank = ps.tile([P, P], F32, name="fade_col_bank", tag="back00")
        nc.tensor.transpose(bank[:], fade_rows[:], ident[:])
        nc.scalar.copy(fade_col[:], bank[:, 0:8])
        turned = sb.tile([P, 8, 2, P], F32, name="turned", tag="turned")
        for pair, tag in enumerate(("prod2", "prod3", "back01", "back11")):
            bank = ps.tile([P, 2, 2, P], F32, name=f"old_bank{pair}", tag=tag)
            for u in range(2):
                b = 2 * pair + u
                for j in range(2):
                    nc.tensor.transpose(bank[:, u, j, :], old_sb[2 + j][:, b * P : (b + 1) * P], ident[:])
            for u in range(2):
                b = 2 * pair + u
                nc.scalar.activation(turned[:, b], bank[:, u, :, :], ACT.Copy, scale=fade_col[:, b : b + 1])
        faded = {}
        for h in range(2):
            for j in range(2):
                bank = ps.tile([P, 4, P], F32, name=f"faded{j}{h}", tag=f"back{j}{h}")
                faded[j, h] = bank
                for x in range(4):
                    nc.tensor.transpose(bank[:, x, :], turned[:, 4 * h + x, j, :], ident[:])

        turned1 = sb.tile([P, 4, P], F32, name="turned1")
        faded1 = sb.tile([P, BANK], F32, name="faded1", tag="faded1")
        bank = ps.tile([P, 4, P], F32, name="old1_bank", tag="prod2")
        for x in range(4):
            nc.tensor.transpose(bank[:, x, :], old_sb[1][:, BANK + x * P : BANK + (x + 1) * P], ident[:])
        for x in range(4):
            nc.scalar.activation(turned1[:, x, :], bank[:, x, :], ACT.Copy, scale=fade_col[:, 4 + x : 5 + x])
        bank = ps.tile([P, 4, P], F32, name="faded1_bank", tag="prod3")
        for x in range(4):
            nc.tensor.transpose(bank[:, x, :], turned1[:, x, :], ident[:])
        nc.scalar.copy(faded1[:], bank[:].rearrange("p x n -> p (x n)"))

        def scatter(j):
            nc.vector.tensor_copy(gf[j][:].indirect(offs_sb[:]), gv[j])

        def finish_vector(j, res):
            for h in range(2):
                cols = slice(h * BANK, (h + 1) * BANK)
                nc.vector.tensor_tensor(res[:, cols], faded[j - 2, h][:].rearrange("p x n -> p (x n)"), gf[j][:, cols], ALU.add)
                nc.sync.dma_start(out[j * P : (j + 1) * P, cols], res[:, cols])

        faded0 = sb.tile([P, T], F32, name="faded0", tag="win3", align_bytes=64)
        res0 = sb.tile([P, T], F32, name="res0")
        nc.gpsimd.tensor_tensor(faded0[:], old_sb[0][:], fade_all[:], ALU.mult)
        scatter(0)
        nc.gpsimd.tensor_tensor(res0[:], faded0[:], gf[0][:], ALU.add)
        nc.sync.dma_start(out[0:P, :], res0[:])
        late = sb.tile([P, T + I + BANK], F32, name="late", tag="win3", align_bytes=64)
        res2, faded1_low = late[:, :T], late[:, T + I :]
        gv.append(late[:, T : T + I])
        gradient(3, slice(0, I), "prod1")
        scatter(1)
        scatter(2)
        finish_vector(2, res2)
        nc.gpsimd.tensor_tensor(faded1_low, old_sb[1][:, :BANK], fade_all[:, :BANK], ALU.mult)
        res1_high = sb.tile([P, BANK], F32, name="res1_high")
        nc.gpsimd.tensor_tensor(res1_high[:], faded1[:], gf[1][:, BANK:], ALU.add)
        nc.scalar.dma_start(out[P : 2 * P, BANK:], res1_high[:])
        res1_low = sb.tile([P, BANK], F32, name="res1_low", tag="faded1")
        nc.gpsimd.tensor_tensor(res1_low[:], faded1_low, gf[1][:, :BANK], ALU.add)
        nc.scalar.dma_start(out[P : 2 * P, :BANK], res1_low[:])
        scatter(3)
        res3 = sb.tile([P, T], F32, name="res3")
        finish_vector(3, res3[:])
